import numpy as np
import ml_dtypes


def mxq(x, axis, fmt="e4m3"):
    dtype, down = {"e4m3": (ml_dtypes.float8_e4m3fn, 7), "e5m2": (ml_dtypes.float8_e5m2, 14)}[fmt]
    v = np.moveaxis(np.asarray(x, np.float32).astype(ml_dtypes.bfloat16).astype(np.float64), axis, -1)
    blocks = v.reshape(v.shape[:-1] + (-1, 32))
    amax = np.abs(blocks).max(-1, keepdims=True)
    byte = np.maximum(np.where(amax > 0, np.frexp(amax)[1] - 1 + 127, 0) - down, 1)
    scale = np.exp2(byte - 127.0)
    codes = (blocks / scale).astype(np.float32).astype(dtype).astype(np.float64)
    return np.moveaxis((codes * scale).reshape(v.shape), -1, axis)


WIDE = False


def mx_kscale(k):
    if not WIDE:
        return np.ones(k)
    levels = np.array([10, -10, 5, -5, 0])
    if k % 512:
        return np.exp2(np.random.permutation(np.resize(levels, k // 32))).repeat(32)
    a = np.empty((k // 512, 16))
    for p in range(k // 512):
        a[p, :8] = np.random.permutation(np.resize(levels, 8))
        for g in range(8):
            far = levels[np.abs(levels - a[p, g]) >= 10]
            a[p, g + 8] = far[np.random.randint(len(far))]
    return np.exp2(a.ravel()).repeat(32)


BF16 = ml_dtypes.bfloat16


def bf(x):
    return np.asarray(x, np.float32).astype(BF16)


def f64(x):
    return np.asarray(x).astype(np.float64)


Q, N, D, T = 8192, 512, 512, 128

LOG_AMPLITUDE = 8.4
DIST_SCALE = 128.0

XS = np.sqrt(4.0 * DIST_SCALE / D)


def draw0():
    s, t = mx_kscale(D), mx_kscale(N)
    x = bf(np.random.standard_normal((Q, D)) * XS * s)
    zt = bf(np.random.standard_normal((N, D)) * XS / s)
    lam = bf(np.random.uniform(0.5, 1.5, D) / (s * s))
    c = bf(np.random.standard_normal(N) * t)
    alpha = bf(np.random.standard_normal((N, T)) / np.sqrt(N) / t[:, None])
    beta = bf(np.random.standard_normal((D, T)) / (XS * np.sqrt(D)) / s[:, None])
    return {"x": x, "zt": zt, "lam": lam, "c": c, "alpha": alpha, "beta": beta}


def core(x, zt, lam, c, alpha, beta):
    x, zt, lam, c = f64(x), f64(zt), f64(lam), f64(c)
    nx = np.sum(lam[None, :] * np.square(x), axis=1)
    nz = np.sum(np.square(zt) / lam[None, :], axis=1)
    xq = mxq(x, 1, "e4m3")
    dot = xq @ mxq(zt, 1, "e4m3").T
    k = np.exp(LOG_AMPLITUDE - (nx[:, None] + nz[None, :] - 2.0 * dot) / DIST_SCALE)
    kc = k * c[None, :]
    lin = xq @ mxq(f64(beta), 0, "e4m3")
    return lin + (mxq(kc, 1, "e4m3") @ mxq(f64(alpha), 0, "e4m3"))


def e4m3fn_bytes(y):
    return np.clip(np.asarray(y, np.float64), -448.0, 448.0).astype(np.float32).astype(ml_dtypes.float8_e4m3fn).view(np.uint8)


def e4m3fn_values(b):
    return np.asarray(b, np.uint8).view(ml_dtypes.float8_e4m3fn).astype(np.float64)


def setup_inputs():
    d = draw0()
    x0 = np.asarray(d['beta']).astype(np.float64)
    s = (np.max(np.abs(x0), axis=(1,), keepdims=True) / 448.0).astype(np.float32)
    out = {}
    for k, v in d.items():
        if k == 'beta':
            out['beta_bytes'] = e4m3fn_bytes(x0 / s.astype(np.float64))
            out['beta_scale'] = s
        else:
            out[k] = v
    return out


def reference(x, zt, lam, c, alpha, beta_bytes, beta_scale):
    return core(x, zt, lam, c, alpha, e4m3fn_values(beta_bytes) * beta_scale.astype(np.float64))

from contextlib import ExitStack

import concourse.mybir as mybir
from concourse.masks import make_identity

Q, N, D, T = 8192, 512, 512, 128
P = 128
CHUNK = 512
TILES = CHUNK // P
CHUNKS = Q // CHUNK
ROWS_PER_PARTITION = Q // P

LOG_AMPLITUDE = 8.4
DIST_SCALE = 128.0
HALF_SCALE = DIST_SCALE / 2.0
LN_SPLIT = 2.0**62

ORDER = (
    ("quant_k", -2), ("out_copy", -3), ("empty", 4), ("add", 0), ("square", 4), ("sum_t", 2), ("spread", 1),
    ("sum_p", 2), ("turn", 5), ("spread_copy", 1), ("exp", 0), ("quant_x", 4), ("dot", 1), ("out", -2),
)
FIRST, LAST = -5, 3
Z_AT = (-3, 4)
W_AT = (2, 0)

FLOPS = 2 * Q * N * D + 2 * Q * D * T + 2 * Q * N * T

F32 = mybir.dt.float32
BF16 = mybir.dt.bfloat16
U32 = mybir.dt.uint32
U8 = mybir.dt.uint8
FP8 = mybir.dt.float8_e4m3fn
FP8X4 = mybir.dt.float8_e4m3fn_x4
ALU = mybir.AluOpType
ACT = mybir.ActivationFunctionType
AXIS = mybir.AxisListType


def tile_ardgaussianprocessmean_t_kernel(tc, x, zt, lam, c, alpha, beta_bytes, beta_scale, out):
    nc = tc.nc
    with ExitStack() as ctx:
        sbuf = ctx.enter_context(tc.tile_pool(name="sbuf", bufs=1))
        psum = ctx.enter_context(tc.psum_pool(name="psum", bufs=1))
        ctx.enter_context(tc.manual_schedule())

        x_rows = x.rearrange("(p j) d -> p j d", j=ROWS_PER_PARTITION)
        out_rows = out.rearrange("(p j) t -> p j t", j=ROWS_PER_PARTITION)

        lam_sb = sbuf.tile([P, 4], BF16, name="lam_sb")
        nc.scalar.dma_start(out=lam_sb[:], in_=lam.rearrange("(p t) -> p t", t=4))
        c_sb = sbuf.tile([P, 4], BF16, name="c_sb")
        nc.scalar.dma_start(out=c_sb[:], in_=c.rearrange("(p t) -> p t", t=4))
        z_sb = sbuf.tile([P, TILES, D], BF16, name="z_sb")
        z_view = zt.rearrange("(p j) d -> p j d", j=4)
        for h in range(2):
            nc.sync.dma_start(out=z_sb[:, 2 * h : 2 * h + 2, :], in_=z_view[:, 2 * h : 2 * h + 2, :])
        x_sb = []
        for i in range(CHUNKS):
            xs = sbuf.tile([P, TILES, D], BF16, name="x_sb", bufs=CHUNKS)
            x_sb.append(xs)
            pieces = 2 if i == 0 else 1
            w = TILES // pieces
            for h in range(pieces):
                nc.sync.dma_start(
                    out=xs[:, h * w : (h + 1) * w, :],
                    in_=x_rows[:, TILES * i + h * w : TILES * i + (h + 1) * w, :],
                )
            if i == 1:
                bscale_sb = sbuf.tile([P, 4], F32, name="bscale_sb")
                nc.sync.dma_start(out=bscale_sb[:], in_=beta_scale.rearrange("(p t) o -> p (t o)", t=4))
                beta_u8 = sbuf.tile([P, 4, T], U8, name="beta_u8")
                nc.sync.dma_start(out=beta_u8[:], in_=beta_bytes.rearrange("(p t) n -> p t n", t=4))
                alpha_sb = sbuf.tile([P, 4, T], BF16, name="alpha_sb")
                nc.sync.dma_start(out=alpha_sb[:], in_=alpha.rearrange("(p t) n -> p t n", t=4))

        ident = sbuf.tile([P, P], F32, name="ident")
        make_identity(nc, ident[:])
        half = sbuf.tile([P, 4], F32, name="half")
        nc.gpsimd.memset(half[:], 0.5)
        mhalf = sbuf.tile([P, 4], F32, name="mhalf")
        nc.gpsimd.memset(mhalf[:], -0.5)

        lam_half = sbuf.tile([P, 4], F32, name="lam_half")
        nc.vector.tensor_scalar(out=lam_half[:], in0=lam_sb[:], scalar1=0.5, scalar2=None, op0=ALU.mult)
        lam_two = sbuf.tile([P, 4], F32, name="lam_two")
        nc.vector.tensor_scalar(out=lam_two[:], in0=lam_sb[:], scalar1=2.0, scalar2=None, op0=ALU.mult)
        z_factor = sbuf.tile([P, 4], F32, name="z_factor")
        nc.gpsimd.tensor_tensor(out=z_factor[:], in0=lam_two[:], in1=mhalf[:], op=ALU.pow)
        x_factor = sbuf.tile([P, 4], F32, name="x_factor")
        nc.gpsimd.tensor_tensor(out=x_factor[:], in0=lam_half[:], in1=half[:], op=ALU.pow)

        c_abs = sbuf.tile([P, 4], F32, name="c_abs")
        nc.vector.scalar_tensor_tensor(out=c_abs[:], in0=c_sb[:], scalar=-1.0, in1=c_sb[:], op0=ALU.mult, op1=ALU.max)
        c_lim = sbuf.tile([P, 4], F32, name="c_lim")
        nc.vector.tensor_scalar(
            out=c_lim[:], in0=c_abs[:], scalar1=LN_SPLIT**-2, scalar2=LN_SPLIT**2, op0=ALU.max, op1=ALU.min
        )
        c_parts = sbuf.tile([P, 3, 4], F32, name="c_parts")
        nc.vector.tensor_scalar(
            out=c_parts[:, 0, :], in0=c_lim[:], scalar1=1.0 / LN_SPLIT, scalar2=LN_SPLIT, op0=ALU.max, op1=ALU.min
        )
        nc.vector.tensor_scalar(
            out=c_parts[:, 1, :], in0=c_lim[:], scalar1=1.0 / LN_SPLIT, scalar2=1.0, op0=ALU.mult, op1=ALU.max
        )
        nc.vector.tensor_scalar(
            out=c_parts[:, 2, :], in0=c_lim[:], scalar1=LN_SPLIT, scalar2=1.0, op0=ALU.mult, op1=ALU.min
        )
        c_logs = sbuf.tile([P, 3, 4], F32, name="c_logs")
        nc.scalar.activation(out=c_logs[:], in_=c_parts[:], func=ACT.Ln)
        warm = sbuf.tile([P, 1], F32, name="warm")
        nc.scalar.activation(out=warm[:], in_=half[:, 0:1], func=ACT.Exp)
        c_sign = sbuf.tile([P, 4], F32, name="c_sign")
        nc.vector.tensor_scalar(out=c_sign[:], in0=c_sb[:], scalar1=0.0, scalar2=2.0, op0=ALU.is_ge, op1=ALU.mult)
        c_sign1 = sbuf.tile([P, 4], F32, name="c_sign1")
        nc.vector.tensor_scalar(out=c_sign1[:], in0=c_sign[:], scalar1=-1.0, scalar2=None, op0=ALU.add)
        c_log = sbuf.tile([P, 4], F32, name="c_log")
        c_log2 = sbuf.tile([P, 4], F32, name="c_log2")
        c_log3 = sbuf.tile([P, 4], F32, name="c_log3")
        bias = sbuf.tile([P, 4], F32, name="bias")

        def turn(rows):
            banks = []
            for b in range(2):
                bank = psum.tile([P, 2, 2, P], F32, name="xt", bufs=2)
                for jj in range(2):
                    words = rows[:, 2 * b + jj, :].bitcast(F32)
                    for u in range(2):
                        nc.tensor.transpose(bank[:, jj, u, :], words[:, u::2], ident[:])
                banks.append(bank)
            return banks

        def empty(banks):
            grouped = sbuf.tile([P, CHUNK, 2], F32, name="grouped", bufs=3, align_bytes=64)
            for b in range(2):
                nc.vector.tensor_copy(
                    out=grouped[:, 2 * P * b : 2 * P * (b + 1), :].rearrange("p (j r) u -> p j r u", j=2),
                    in_=banks[b][:].rearrange("p j u r -> p j r u"),
                )
            return grouped[:].rearrange("p q u -> p (q u)").bitcast(BF16)

        def quantise(flat, what, bufs):
            w = flat.shape[1] // 4
            codes = sbuf.tile([P, w], U32, name=what + "_codes", bufs=bufs, align_bytes=64)
            scales = sbuf.tile([P, w], U8, name=what + "_scales", bufs=bufs, align_bytes=64)
            nc.vector.quantize_mx(out=codes[:].bitcast(FP8X4), scales=scales[:], in_=flat)
            return codes, scales

        def squares(flat, sq, factor, ts):
            cols = flat.rearrange("p (q t) -> p q t", t=4)
            for t in ts:
                nc.scalar.activation(out=sq[:, t, :], in_=cols[:, :, t], func=ACT.Square, scale=factor[:, t : t + 1])

        def squares_gpsimd(flat, sq, t):
            cols = flat.rearrange("p (q t) -> p q t", t=4)
            y = sbuf.tile([P, CHUNK], F32, name="y", bufs=2)
            nc.gpsimd.tensor_scalar(
                out=y[:], in0=cols[:, :, t], scalar1=lam_half[:, t : t + 1], scalar2=0.0, op0=ALU.mult, op1=ALU.add
            )
            nc.gpsimd.tensor_tensor(out=sq[:, t, :], in0=y[:], in1=cols[:, :, t], op=ALU.mult)

        def sum_t(sq):
            bank = psum.tile([P, TILES, P], F32, name="misc", bufs=2)
            for j in range(TILES):
                for t in range(4):
                    nc.tensor.matmul(
                        out=bank[:, j, :],
                        lhsT=sq[:, t, P * j : P * (j + 1)],
                        rhs=ident[:],
                        is_transpose=True,
                        start=(t == 0),
                        stop=(t == 3),
                    )
            return bank

        def sum_p(bank):
            n = sbuf.tile([P, TILES], F32, name="norms", bufs=4)
            nc.vector.tensor_reduce(out=n[:], in_=bank[:], axis=AXIS.X, op=ALU.add)
            return n

        def spread(n):
            bank = psum.tile([P, TILES, P], F32, name="misc", bufs=2)
            for j in range(TILES):
                nc.tensor.transpose(bank[:, j, :], n[:, j : j + 1].to_broadcast([P, P]), ident[:])
            return bank

        z_banks = turn(z_sb)
        z_flat = empty(z_banks)
        z_sq = sbuf.tile([P, 4, CHUNK], F32, name="sq", bufs=3)
        squares(z_flat, z_sq, z_factor, range(4))
        z_codes, z_scales = quantise(z_flat, "z", 1)

        def finish_z():
            n = sum_p(sum_t(z_sq))
            nc.vector.tensor_tensor(out=c_log[:], in0=c_logs[:, 0, :], in1=c_logs[:, 1, :], op=ALU.add)
            nc.vector.tensor_tensor(out=c_log2[:], in0=c_log[:], in1=c_logs[:, 2, :], op=ALU.add)
            nc.vector.tensor_scalar(
                out=c_log3[:],
                in0=c_log2[:],
                scalar1=HALF_SCALE,
                scalar2=HALF_SCALE * LOG_AMPLITUDE,
                op0=ALU.mult,
                op1=ALU.add,
            )
            nc.vector.tensor_tensor(out=bias[:], in0=c_log3[:], in1=n[:], op=ALU.subtract)
            return bias

        def weights():
            wide = sbuf.tile([P, 4, T], F32, name="wide")
            nc.gpsimd.tensor_copy(out=wide[:], in_=beta_u8[:].bitcast(FP8))
            both = sbuf.tile([P, 2 * T, 4], BF16, name="both", align_bytes=64)
            nc.vector.tensor_tensor(
                out=both[:, 0:T, :],
                in0=wide[:].rearrange("p t n -> p n t"),
                in1=bscale_sb[:].unsqueeze(1).to_broadcast([P, T, 4]),
                op=ALU.mult,
            )
            nc.vector.tensor_tensor(
                out=both[:, T : 2 * T, :],
                in0=alpha_sb[:].rearrange("p t n -> p n t"),
                in1=c_sign1[:].unsqueeze(1).to_broadcast([P, T, 4]),
                op=ALU.mult,
            )
            return quantise(both[:].rearrange("p n t -> p (n t)"), "w", 1)

        xt, flat, sqs, tsums, norms, nbank, nxb, xq, dots, args, kgs, kq, ob = ({} for _ in range(13))
        wq = {}

        def s_turn(i):
            xt[i] = turn(x_sb[i])

        def s_empty(i):
            flat[i] = empty(xt[i])
            sqs[i] = sbuf.tile([P, 4, CHUNK], F32, name="sq", bufs=3)
            squares_gpsimd(flat[i], sqs[i], 3)

        def s_square(i):
            squares(flat[i], sqs[i], x_factor, range(3))

        def s_quant_x(i):
            xq[i] = quantise(flat[i], "x", 8)

        def s_sum_t(i):
            tsums[i] = sum_t(sqs[i])

        def s_sum_p(i):
            norms[i] = sum_p(tsums[i])

        def s_spread(i):
            nbank[i] = spread(norms[i])

        def s_spread_copy(i):
            nxb[i] = sbuf.tile([P, CHUNK], F32, name="nxb", bufs=3)
            nc.scalar.copy(out=nxb[i][:], in_=nbank[i][:].rearrange("p j r -> p (j r)"))

        def s_dot(i):
            dots[i] = []
            for t in range(4):
                bank = psum.tile([P, CHUNK], F32, name="dot", bufs=4)
                nc.tensor.matmul_mx(
                    out=bank[:],
                    lhsT=z_codes[:, P * t : P * (t + 1)].bitcast(FP8X4),
                    lhsT_scale=z_scales[:, P * t : P * (t + 1)],
                    rhs=xq[i][0][:].bitcast(FP8X4),
                    rhs_scale=xq[i][1][:],
                    start=True,
                    stop=True,
                )
                dots[i].append(bank)

        def s_add(i):
            args[i] = sbuf.tile([P, 4, CHUNK], F32, name="arg", bufs=2)
            for t in range(4):
                nc.vector.scalar_tensor_tensor(
                    out=args[i][:, t, :],
                    in0=dots[i][t][:],
                    scalar=wq["bias"][:, t : t + 1],
                    in1=nxb[i][:],
                    op0=ALU.add,
                    op1=ALU.subtract,
                )

        def s_exp(i):
            kgs[i] = sbuf.tile([P, CHUNK, 4], BF16, name="kg", bufs=2, align_bytes=64)
            nc.scalar.activation(
                out=kgs[i][:].rearrange("p (c i) t -> p c t i", i=4),
                in_=args[i][:].rearrange("p t (c i) -> p c t i", i=4),
                func=ACT.Exp,
                scale=1.0 / HALF_SCALE,
            )

        def s_quant_k(i):
            kq[i] = quantise(kgs[i][:].rearrange("p q t -> p (q t)"), "k", 3)

        def s_out(i):
            ob[i] = psum.tile([P, TILES, T], F32, name="misc", bufs=2)
            w_codes, w_scales = wq[0]
            for j in range(TILES):
                cols = slice(P * j, P * (j + 1))
                for s, (codes, scales) in enumerate((xq[i], kq[i])):
                    nc.tensor.matmul_mx(
                        out=ob[i][:, j, :],
                        lhsT=codes[:, cols].bitcast(FP8X4),
                        lhsT_scale=scales[:, cols],
                        rhs=w_codes[:, T * s : T * (s + 1)].bitcast(FP8X4),
                        rhs_scale=w_scales[:, T * s : T * (s + 1)],
                        start=(s == 0),
                        stop=(s == 1),
                    )

        def s_out_copy(i):
            o_sb = sbuf.tile([P, TILES, T], F32, name="o_sb", bufs=3)
            nc.scalar.copy(out=o_sb[:], in_=ob[i][:])
            nc.sync.dma_start(out=out_rows[:, TILES * i : TILES * (i + 1), :], in_=o_sb[:])

        steps = {
            "turn": s_turn, "empty": s_empty, "square": s_square, "quant_x": s_quant_x, "sum_t": s_sum_t,
            "sum_p": s_sum_p, "spread": s_spread, "spread_copy": s_spread_copy, "dot": s_dot, "add": s_add,
            "exp": s_exp, "quant_k": s_quant_k, "out": s_out, "out_copy": s_out_copy,
        }
        for i in range(FIRST, CHUNKS + LAST):
            for at, (name, ahead) in enumerate(ORDER):
                if 0 <= i + ahead < CHUNKS:
                    steps[name](i + ahead)
                if (i, at) == Z_AT:
                    wq["bias"] = finish_z()
                if (i, at) == W_AT:
                    wq[0] = weights()
